import numpy as np, ml_dtypes
CORES = [10,14,66,70,74,78,82,86,90,94,106,110]
N = 12
TOK, K, FT = 32, 3, 2
ROUTE = [[[5,8,10],[3,5,8],[1,4,10],[0,6,7],[1,2,6],[3,4,9],[0,8,10],[0,7,8],[2,7,8],[1,6,9],[0,7,9],[3,6,11],[5,6,8],[4,6,10],[4,5,7],[0,1,6],[3,5,11],[3,7,9],[0,2,5],[0,5,6],[0,1,4],[4,6,7],[5,7,10],[6,10,11],[3,7,10],[4,5,11],[5,9,11],[5,9,11],[1,5,7],[8,10,11],[6,8,10],[1,9,10]],[[3,5,11],[4,10,11],[7,8,9],[4,6,8],[6,9,11],[2,6,9],[0,5,6],[2,4,11],[1,6,10],[2,5,9],[4,9,11],[0,6,10],[3,9,11],[0,1,4],[7,9,11],[1,6,10],[4,6,9],[1,7,11],[3,6,8],[4,9,11],[6,7,8],[0,2,3],[4,5,11],[5,7,10],[4,6,10],[1,3,6],[0,2,9],[6,9,11],[4,7,11],[1,5,7],[6,7,10],[0,2,8]],[[2,4,10],[8,9,11],[4,5,6],[1,2,8],[0,4,6],[0,2,10],[1,9,11],[0,1,3],[1,3,4],[0,6,11],[1,4,9],[2,6,9],[3,6,7],[8,9,11],[5,8,10],[0,2,5],[7,8,9],[0,7,8],[0,10,11],[4,6,7],[2,6,10],[1,5,10],[2,6,9],[3,5,11],[1,6,7],[0,4,5],[5,7,8],[2,6,9],[1,2,3],[0,1,5],[2,5,9],[0,2,9]],[[0,4,6],[4,9,10],[7,9,10],[1,7,9],[1,7,9],[1,4,10],[6,8,11],[2,7,9],[5,7,10],[0,4,7],[1,4,7],[5,7,9],[0,3,11],[7,10,11],[0,3,5],[4,7,8],[1,2,8],[4,5,7],[5,6,11],[4,6,8],[7,9,10],[2,10,11],[0,5,10],[4,5,8],[3,7,9],[1,4,10],[1,9,10],[3,7,8],[0,10,11],[0,7,9],[2,4,11],[3,4,10]],[[0,1,5],[7,9,11],[4,6,8],[1,2,7],[1,2,6],[0,5,8],[3,10,11],[6,7,9],[1,8,11],[0,2,8],[1,3,5],[3,8,9],[0,4,9],[6,8,9],[0,7,10],[3,5,11],[1,6,7],[5,7,10],[2,7,10],[6,7,11],[1,4,10],[2,5,11],[1,3,4],[4,5,10],[0,7,9],[2,6,7],[2,5,9],[2,8,11],[4,6,8],[0,2,5],[0,7,11],[3,5,10]],[[5,6,11],[1,6,11],[7,8,11],[3,4,6],[1,2,7],[0,4,10],[1,2,7],[7,9,11],[0,4,5],[1,6,7],[1,5,11],[2,9,11],[0,7,9],[3,7,8],[2,5,11],[4,7,11],[8,9,11],[0,1,3],[1,10,11],[0,4,9],[5,8,11],[3,6,10],[1,2,3],[0,2,6],[3,5,11],[2,3,6],[5,6,10],[0,3,4],[4,6,7],[2,4,11],[7,10,11],[2,4,6]],[[4,6,7],[0,2,5],[2,8,11],[3,5,10],[0,8,10],[3,4,10],[1,4,6],[1,8,9],[0,6,8],[1,2,4],[1,2,5],[5,6,7],[0,2,6],[1,4,5],[1,8,10],[2,4,5],[1,9,10],[5,8,10],[1,3,4],[3,6,8],[0,3,4],[3,5,9],[2,8,9],[0,2,3],[0,1,6],[6,10,11],[2,3,6],[4,6,7],[0,4,7],[7,8,9],[0,2,5],[0,1,6]],[[5,10,11],[0,7,9],[5,8,11],[3,8,9],[2,5,9],[5,6,7],[1,9,11],[3,4,10],[3,7,9],[0,5,9],[0,2,7],[4,6,8],[2,8,11],[2,8,9],[1,4,5],[1,5,10],[1,3,4],[0,1,3],[2,4,10],[4,5,6],[5,9,10],[1,5,11],[5,8,9],[4,5,7],[3,4,6],[1,5,6],[0,8,9],[0,6,8],[2,5,10],[7,8,11],[2,3,6],[0,3,7]],[[2,3,7],[1,3,11],[4,8,9],[4,5,11],[1,4,9],[1,3,6],[2,4,6],[9,10,11],[0,1,4],[6,7,8],[7,9,11],[0,5,9],[4,5,6],[1,3,11],[6,7,11],[2,6,9],[0,5,8],[2,6,8],[5,9,10],[0,7,10],[0,3,5],[4,9,11],[1,5,7],[1,7,11],[2,3,6],[3,6,10],[5,7,11],[4,6,11],[0,5,8],[4,5,7],[5,7,11],[3,6,10]],[[0,4,10],[0,4,11],[2,7,11],[3,4,5],[2,8,10],[1,4,11],[3,7,8],[2,3,7],[4,7,11],[2,3,9],[2,4,8],[2,9,10],[3,4,10],[0,7,8],[0,5,8],[2,3,6],[6,7,9],[4,6,9],[3,5,11],[4,5,7],[0,2,6],[1,2,5],[2,6,11],[1,4,7],[1,5,9],[0,1,6],[1,7,11],[1,9,10],[5,8,11],[2,7,8],[0,8,11],[0,4,9]],[[2,8,10],[2,6,9],[1,4,8],[1,4,5],[0,4,9],[1,4,9],[1,7,9],[3,4,11],[3,5,7],[1,6,8],[7,9,10],[4,7,10],[2,5,6],[4,6,8],[0,4,5],[3,8,11],[3,6,8],[6,7,8],[0,8,10],[0,5,6],[0,1,9],[2,3,8],[5,8,10],[2,9,10],[0,1,2],[3,6,8],[3,8,10],[0,1,2],[1,5,6],[3,4,9],[0,6,11],[0,2,6]],[[1,5,10],[0,7,8],[4,5,7],[5,9,10],[0,3,8],[0,6,8],[0,4,8],[3,7,9],[0,2,11],[6,7,8],[7,9,10],[1,6,9],[2,3,6],[2,5,8],[5,8,9],[3,9,10],[4,5,6],[1,3,5],[2,6,11],[3,4,8],[5,6,9],[0,7,10],[4,5,9],[0,3,7],[0,4,10],[0,4,11],[6,7,11],[3,5,9],[4,5,6],[1,8,11],[4,9,10],[2,6,7]]]
def setup_inputs(rng):
    return {"x": rng.standard_normal((N, 128, TOK), dtype=np.float32).astype(ml_dtypes.bfloat16), "gate": (0.5 * rng.integers(1, 4, size=(N, K, TOK)) * (2 * rng.integers(0, 2, size=(N, K, TOK)) - 1)).astype(np.float32).astype(ml_dtypes.bfloat16), "w1": (rng.standard_normal((N, 128, FT * 128), dtype=np.float32) / 8).astype(ml_dtypes.bfloat16), "w2": (rng.standard_normal((N, 128, FT * 128), dtype=np.float32) / 8).astype(ml_dtypes.bfloat16)}
def setup_inputs_big(rng):
    d = setup_inputs(rng)
    for k in ("x", "gate", "w1", "w2"): d[k] = (d[k].astype(np.float32) * 1024.0).astype(d[k].dtype)
    return d
def setup_inputs_small(rng):
    d = setup_inputs(rng)
    for k in ("x", "gate", "w1", "w2"): d[k] = (d[k].astype(np.float32) * (1 / 1024.0)).astype(d[k].dtype)
    return d
def reference(x, gate, w1, w2):
    X, GATE, W1, W2 = x.astype(np.float64), gate.astype(np.float64), w1.astype(np.float64), w2.astype(np.float64)
    y = np.zeros((N, 128, TOK))
    for r in range(N):
        for t in range(TOK):
            for i, e in enumerate(ROUTE[r][t]):
                hid = np.maximum(W1[e].T @ X[r][:, t], 0.0)
                y[r][:, t] += GATE[r][i, t] * sum(W2[e][:, 128 * f:128 * f + 128].T @ hid[128 * f:128 * f + 128] for f in range(FT))
    return {"y": y.astype(ml_dtypes.bfloat16)}

@@ -1,0 +1,252 @@
+from concourse.bass import DstId, RemoteDMATransfer
+from concourse.mybir import AluOpType
+
+NS = 6
+TOKS = 32
+
+SCRATCH = {
+    "X": ("sbuf", [128, NS * 32], "bfloat16"),
+    "W1": ("sbuf", [128, 512], "bfloat16"),
+    "W2": ("sbuf", [128, 512], "bfloat16"),
+    "g1": ("sbuf", [128, 96], "bfloat16"),
+    "ones": ("sbuf", [128, 128], "bfloat16"),
+    "zeros": ("sbuf", [128, 256], "float32"),
+    "HsA": ("sbuf", [128, 192], "bfloat16"),
+    "HsB": ("sbuf", [128, 192], "bfloat16"),
+    "HsC": ("sbuf", [128, 256], "bfloat16"),
+    "HsD": ("sbuf", [128, 128], "bfloat16"),
+    "Z": ("sbuf", [128, NS * 64], "bfloat16"),
+    "R": ("sbuf", [128, NS * 64], "bfloat16"),
+    "P": ("sbuf", [128, NS * 64], "float32"),
+    "ACC": ("sbuf", [128, NS * 64], "float32"),
+    "Y": ("sbuf", [128, 32], "bfloat16"),
+    "G": ("psum", [128, 512], "float32"),
+    "HA": ("psum", [128, 512], "float32"),
+    "HB": ("psum", [128, 512], "float32"),
+    "HC": ("psum", [128, 512], "float32"),
+    "HD": ("psum", [128, 512], "float32"),
+    "ZE": ("psum", [128, 512], "float32"),
+    "ZF": ("psum", [128, 512], "float32"),
+    "ZG": ("psum", [128, 512], "float32"),
+}
+SEMAPHORES = (["x_ld", "w1_ld", "w2_ld", "g_ld", "y_st", "vin", "zr", "gdone", "wp1", "wp2", "sent",
+               "m1A", "m1B", "m1C", "m1D", "rlA", "rlB", "rlC", "rlD", "m2E", "m2F", "m2G",
+               "cpE", "cpF", "cpG", "cp0"]
+              + ["xs%d" % i for i in range(NS)] + ["rs%d" % i for i in range(NS)]
+              + ["pk%d" % i for i in range(NS)] + ["ac%d" % i for i in range(NS + 2)])
+
+
+def _bits(mask):
+    return [b for b in range(16) if (mask >> b) & 1]
+
+
+def _mk(bits):
+    m = 0
+    for b in bits:
+        m |= 1 << b
+    return m
+
+
+def _layout(T, topo):
+    chips = sorted(set(topo.chip(c) for c in T.cores))
+    first = [c for c in T.cores if topo.chip(c) == chips[0]]
+    dies = [topo.die(c) for c in first]
+    members = []
+    for ch in chips:
+        row = [None] * len(dies)
+        for r, c in enumerate(T.cores):
+            if topo.chip(c) == ch:
+                row[dies.index(topo.die(c))] = r
+        members.append(row)
+    return members
+
+
+def _scatter_plan(route_r, blk):
+    plan, singles = [], {}
+    for t, es in enumerate(route_r):
+        c = [blk[e] * TOKS + t for e in es]
+        d0, d1 = c[1] - c[0], c[2] - c[1]
+        if d0 == d1 and d0 > 0:
+            plan.append(((t, t + 65, 32), (c[0], c[2] + 1, d0)))
+        elif d0 > 0:
+            plan.append(((t, t + 33, 32), (c[0], c[1] + 1, d0)))
+            singles[(2, t)] = c[2]
+        elif d1 > 0:
+            plan.append(((32 + t, 32 + t + 33, 32), (c[1], c[2] + 1, d1)))
+            singles[(0, t)] = c[0]
+        else:
+            for i in range(3):
+                singles[(i, t)] = c[i]
+    done = set()
+    for (i, t) in sorted(singles):
+        if (i, t) in done:
+            continue
+        n = 1
+        while (i, t + n) in singles and singles[(i, t + n)] == singles[(i, t)] + n:
+            n += 1
+        for q in range(n):
+            done.add((i, t + q))
+        plan.append(((i * 32 + t, i * 32 + t + n, 1), (singles[(i, t)], singles[(i, t)] + n, 1)))
+    return plan
+
+
+def rank_program(g, core, T, topo):
+    rank = T.rank_of(core)
+    if rank is None:
+        return
+    S = T.sem
+    pe, ve = g.tensor, g.vector
+    members = _layout(T, topo)
+    s = [i for i, row in enumerate(members) if rank in row][0]
+    lane = members[s].index(rank)
+    other = 1 - lane
+    partner = T.cores[members[s][other]]
+    blk = {}
+    for i, row in enumerate(members):
+        for j, r in enumerate(row):
+            blk[r] = i * 2 + j
+    site_core = [T.cores[members[i][lane]] for i in range(NS)]
+
+    off = topo.mask(core, partner)
+    for i in range(NS):
+        if i != s:
+            off &= topo.mask(core, site_core[i])
+    on = topo.mask(core, partner) & ~off
+    if on == 0:
+        on = topo.mask(core, partner)
+    ob = _bits(off)
+    halves = [_mk(ob[:len(ob) // 2]), _mk(ob[len(ob) // 2:])]
+    n_off, n_on, n_half = len(ob), len(_bits(on)), len(ob) // 2
+
+    def dst_id(c):
+        rid, pid, _ = topo.addr(c)
+        return DstId(rid=rid, pnc=pid)
+
+    own_c, oth_c = lane * 256, other * 256
+
+    g.sync.dma_start(T.X[:, 0:32], T.x[:]).then_inc(S.x_ld, 16)
+    g.scalar.dma_start(T.g1[0:1, :], T.gate[:]).then_inc(S.g_ld, 16)
+    g.sync.dma_start(T.W1[:, own_c:own_c + 256], T.w1[:]).then_inc(S.w1_ld, 16)
+    g.scalar.dma_start(T.W2[:, own_c:own_c + 256], T.w2[:]).then_inc(S.w2_ld, 16)
+
+    ve.memset(T.ones[0:1, :], 1.0).then_inc(S.vin, 1)
+    ve.memset(T.G[:, 0:NS * 64], 0.0).then_inc(S.vin, 1)
+    ve.memset(T.zeros[:], 0.0).then_inc(S.zr, 1)
+
+    sent = 0
+    g.wait_ge(S.x_ld, 16)
+    ks = list(range(1, NS))
+    g.remote_dma_fused([RemoteDMATransfer(
+        dst_ids=[dst_id(site_core[(s + k) % NS]) for k in ks], dma_engine_mask=off, remote_sem=S["xs%d" % s],
+        srcs=[T.X[:, 0:32]], dsts=[T.X[:, k * 32:(k + 1) * 32] for k in ks])], local_sem=S.sent)
+    sent += n_off
+    prid, ppid, _ = topo.addr(partner)
+    g.wait_ge(S.w1_ld, 16)
+    g.remote_dma(T.W1[:, own_c:own_c + 256], T.W1[:, own_c:own_c + 256], S.wp1, S.sent, ppid, prid, on)
+    sent += n_on
+    g.wait_ge(S.w2_ld, 16)
+    g.remote_dma(T.W2[:, own_c:own_c + 256], T.W2[:, own_c:own_c + 256], S.wp2, S.sent, ppid, prid, on)
+    sent += n_on
+    for sem, pair in ((S.cpE, (1, 2)), (S.cpF, (3, 4))):
+        g.wait_ge(sem, 1)
+        g.remote_dma_fused([RemoteDMATransfer(
+            dst_ids=[dst_id(site_core[(s - k) % NS])], dma_engine_mask=halves[q], remote_sem=S["rs%d" % s],
+            src=T.Z[:, k * 64:(k + 1) * 64], dst=T.R[:, s * 64:(s + 1) * 64]) for q, k in enumerate(pair)],
+            local_sem=S.sent)
+        sent += 2 * n_half
+    g.wait_ge(S.cpG, 1)
+    k = NS - 1
+    rid, pid, _ = topo.addr(site_core[(s - k) % NS])
+    g.remote_dma(T.R[:, s * 64:(s + 1) * 64], T.Z[:, k * 64:(k + 1) * 64], S["rs%d" % s], S.sent, pid, rid, off)
+    sent += n_off
+    g.wait_ge(S.sent, sent)
+
+    plan = _scatter_plan(T.tables["ROUTE"][rank], blk)
+    pe.wait_ge(S.vin, 2)
+    pe.wait_ge(S.g_ld, 16)
+    for (a, b, st), (c0, c1, d) in plan:
+        pe.matmul(T.G[:, c0:c1:d], T.ones[0:1, :], T.g1[0:1, a:b:st], True, True).then_inc(S.gdone, 1)
+
+    def mm1(H, col, wc, x0, n, sem):
+        for f in range(2):
+            pe.matmul(H[:, col + f * n:col + (f + 1) * n], T.W1[:, wc + f * 128:wc + (f + 1) * 128],
+                      T.X[:, x0:x0 + n], True, True).then_inc(sem, 1)
+
+    def mm2(Zp, zcol, wc, Hs, hcol, n, sem):
+        for f in range(2):
+            pe.matmul(Zp[:, zcol:zcol + 32], T.W2[:, wc + f * 128:wc + (f + 1) * 128],
+                      Hs[:, hcol + f * n:hcol + f * n + 32], f == 0, f == 1).then_inc(sem, 1)
+
+    pe.wait_ge(S.x_ld, 16)
+    pe.wait_ge(S.w1_ld, 16)
+    pe.wait_ge(S["xs%d" % ((s - 1) % NS)], n_off)
+    pe.wait_ge(S["xs%d" % ((s - 2) % NS)], n_off)
+    mm1(T.HA, 0, own_c, 0, 96, S.m1A)
+    pe.wait_ge(S.wp1, n_on)
+    mm1(T.HB, 0, oth_c, 0, 96, S.m1B)
+    pe.wait_ge(S.w2_ld, 16)
+    pe.wait_ge(S.rlA, 1)
+    for k in range(3):
+        mm2(T.ZE, k * 64 + lane * 32, own_c, T.HsA, k * 32, 96, S.m2E)
+    pe.wait_ge(S.wp2, n_on)
+    pe.wait_ge(S.rlB, 1)
+    for k in range(3):
+        mm2(T.ZE, k * 64 + other * 32, oth_c, T.HsB, k * 32, 96, S.m2E)
+    pe.wait_ge(S["xs%d" % ((s - 3) % NS)], n_off)
+    pe.wait_ge(S["xs%d" % ((s - 4) % NS)], n_off)
+    for j in range(2):
+        mm1(T.HC, j * 128, j * 256, 96, 64, S.m1C)
+    pe.wait_ge(S.rlC, 1)
+    for k in range(2):
+        for j in range(2):
+            mm2(T.ZF, k * 64 + j * 32, j * 256, T.HsC, j * 128 + k * 32, 64, S.m2F)
+    pe.wait_ge(S["xs%d" % ((s - 5) % NS)], n_off)
+    for j in range(2):
+        mm1(T.HD, j * 64, j * 256, 160, 32, S.m1D)
+    pe.wait_ge(S.rlD, 1)
+    for j in range(2):
+        mm2(T.ZG, j * 32, j * 256, T.HsD, j * 64, 32, S.m2G)
+
+    MAX, MUL, ADD = AluOpType.max, AluOpType.mult, AluOpType.add
+    ve.wait_ge(S.zr, 1)
+    ve.wait_ge(S.m1A, 2)
+    ve.tensor_tensor(T.HsA[:], T.HA[:, 0:192], T.zeros[:, 0:192], MAX).then_inc(S.rlA, 1)
+    ve.wait_ge(S.m1B, 2)
+    ve.tensor_tensor(T.HsB[:], T.HB[:, 0:192], T.zeros[:, 0:192], MAX).then_inc(S.rlB, 1)
+    ve.wait_ge(S.m2E, 12)
+    ve.tensor_copy(T.Z[:, 64:192], T.ZE[:, 64:192]).then_inc(S.cpE, 1)
+    ve.tensor_copy(T.R[:, s * 64:(s + 1) * 64], T.ZE[:, 0:64]).then_inc(S.cp0, 1)
+    ve.wait_ge(S.m1C, 4)
+    ve.tensor_tensor(T.HsC[:], T.HC[:, 0:256], T.zeros[:, 0:256], MAX).then_inc(S.rlC, 1)
+    ve.wait_ge(S.m2F, 8)
+    ve.tensor_copy(T.Z[:, 192:320], T.ZF[:, 0:128]).then_inc(S.cpF, 1)
+    ve.wait_ge(S.m1D, 4)
+    ve.tensor_tensor(T.HsD[:], T.HD[:, 0:128], T.zeros[:, 0:128], MAX).then_inc(S.rlD, 1)
+    ve.wait_ge(S.m2G, 4)
+    ve.tensor_copy(T.Z[:, 320:384], T.ZG[:, 0:64]).then_inc(S.cpG, 1)
+
+    ve.wait_ge(S.gdone, len(plan))
+    ve.wait_ge(S.cp0, 1)
+    for k in range(NS):
+        b = ((s + k) % NS) * 64
+        if k:
+            ve.wait_ge(S["rs%d" % ((s + k) % NS)], n_half if k < NS - 1 else n_off)
+        ve.tensor_tensor(T.P[:, k * 64:(k + 1) * 64], T.R[:, b:b + 64], T.G[:, b:b + 64], MUL).then_inc(S["pk%d" % k], 1)
+        ve.wait_ge(S["pk%d" % k], 1)
+        if 1 <= k < NS - 1:
+            prev = T.P[:, 0:64] if k == 1 else T.ACC[:, (k - 1) * 64:k * 64]
+            if k > 1:
+                ve.wait_ge(S["ac%d" % (k - 1)], 1)
+            ve.tensor_tensor(T.ACC[:, k * 64:(k + 1) * 64], prev, T.P[:, k * 64:(k + 1) * 64], ADD).then_inc(S["ac%d" % k], 1)
+        if k == NS - 2:
+            ve.wait_ge(S["ac%d" % k], 1)
+            ve.tensor_tensor(T.ACC[:, 0:32], T.ACC[:, k * 64:k * 64 + 32], T.ACC[:, k * 64 + 32:k * 64 + 64], ADD).then_inc(S.ac0, 1)
+    k = NS - 1
+    ve.tensor_tensor(T.ACC[:, 32:64], T.P[:, k * 64:k * 64 + 32], T.P[:, k * 64 + 32:k * 64 + 64], ADD).then_inc(S["ac%d" % k], 1)
+    ve.wait_ge(S["ac%d" % k], 1)
+    ve.wait_ge(S.ac0, 1)
+    ve.tensor_tensor(T.Y[:], T.ACC[:, 0:32], T.ACC[:, 32:64], ADD).then_inc(S["ac%d" % NS], 1)
+
+    g.sync.wait_ge(S["ac%d" % NS], 1)
+    g.sync.dma_start(T.y[:], T.Y[:]).then_inc(S.y_st, 16)
+    g.sync.wait_ge(S.y_st, 16)

@@ -3,37 +3,37 @@ from concourse.mybir import AluOpType
 
 NS = 6
 TOKS = 32
+NU = 3
 
 SCRATCH = {
-    "X": ("sbuf", [128, NS * 32], "bfloat16"),
-    "W1": ("sbuf", [128, 512], "bfloat16"),
-    "W2": ("sbuf", [128, 512], "bfloat16"),
+    "X": ("sbuf", [128, NS, 32], "bfloat16"),
+    "W": ("sbuf", [128, 1024], "bfloat16"),
     "g1": ("sbuf", [128, 96], "bfloat16"),
+    "grow": ("sbuf", [128, NS * 64], "bfloat16"),
     "ones": ("sbuf", [128, 128], "bfloat16"),
-    "zeros": ("sbuf", [128, 256], "float32"),
-    "HsA": ("sbuf", [128, 192], "bfloat16"),
-    "HsB": ("sbuf", [128, 192], "bfloat16"),
-    "HsC": ("sbuf", [128, 256], "bfloat16"),
-    "HsD": ("sbuf", [128, 128], "bfloat16"),
-    "Z": ("sbuf", [128, NS * 64], "bfloat16"),
+    "zeros": ("sbuf", [128, 12, 32], "float32"),
+    "zi": ("sbuf", [128, 129], "bfloat16"),
+    "idd": ("dram", [129, 128], "bfloat16"),
+    "ident": ("sbuf", [128, 128], "bfloat16"),
+    "Hs": ("sbuf", [128, NU * 12, 32], "bfloat16"),
+    "Z": ("sbuf", [128, NS, 64], "bfloat16"),
     "R": ("sbuf", [128, NS * 64], "bfloat16"),
-    "P": ("sbuf", [128, NS * 64], "float32"),
-    "ACC": ("sbuf", [128, NS * 64], "float32"),
+    "M": ("sbuf", [128, NS * 64], "bfloat16"),
     "Y": ("sbuf", [128, 32], "bfloat16"),
     "G": ("psum", [128, 512], "float32"),
-    "HA": ("psum", [128, 512], "float32"),
-    "HB": ("psum", [128, 512], "float32"),
-    "HC": ("psum", [128, 512], "float32"),
-    "HD": ("psum", [128, 512], "float32"),
-    "ZE": ("psum", [128, 512], "float32"),
-    "ZF": ("psum", [128, 512], "float32"),
-    "ZG": ("psum", [128, 512], "float32"),
+    "Ha": ("psum", [128, 16, 32], "float32"),
+    "Hb": ("psum", [128, 16, 32], "float32"),
+    "Hc": ("psum", [128, 16, 32], "float32"),
+    "Za": ("psum", [128, 8, 64], "float32"),
+    "Zb": ("psum", [128, 8, 64], "float32"),
+    "Zc": ("psum", [128, 8, 64], "float32"),
+    "AC": ("psum", [128, 512], "float32"),
 }
-SEMAPHORES = (["x_ld", "w1_ld", "w2_ld", "g_ld", "y_st", "vin", "zr", "gdone", "wp1", "wp2", "sent",
-               "m1A", "m1B", "m1C", "m1D", "rlA", "rlB", "rlC", "rlD", "m2E", "m2F", "m2G",
-               "cpE", "cpF", "cpG", "cp0"]
+SEMAPHORES = (["x_ld", "w_ld", "g_ld", "y_st", "vin", "zr", "idm", "id1", "id2", "gsc", "gcp", "gdone", "wp", "sent",
+               "cpown", "acc", "yy"]
+              + ["%s%d" % (n, u) for n in ("m1_", "rl", "m2_", "cp") for u in range(NU)]
               + ["xs%d" % i for i in range(NS)] + ["rs%d" % i for i in range(NS)]
-              + ["pk%d" % i for i in range(NS)] + ["ac%d" % i for i in range(NS + 2)])
+              + ["pk%d" % i for i in range(NS)])
 
 
 def _bits(mask):
@@ -122,42 +122,47 @@ def rank_program(g, core, T, topo):
         rid, pid, _ = topo.addr(c)
         return DstId(rid=rid, pnc=pid)
 
-    own_c, oth_c = lane * 256, other * 256
+    own_c, oth_c = lane * 512, other * 512
+    MAX, MUL = AluOpType.max, AluOpType.mult
+    NG = NS * 64
 
-    g.sync.dma_start(T.X[:, 0:32], T.x[:]).then_inc(S.x_ld, 16)
+    g.sync.dma_start(T.X[:, 0, :], T.x[:]).then_inc(S.x_ld, 16)
     g.scalar.dma_start(T.g1[0:1, :], T.gate[:]).then_inc(S.g_ld, 16)
-    g.sync.dma_start(T.W1[:, own_c:own_c + 256], T.w1[:]).then_inc(S.w1_ld, 16)
-    g.scalar.dma_start(T.W2[:, own_c:own_c + 256], T.w2[:]).then_inc(S.w2_ld, 16)
+    g.sync.dma_start(T.W[:, own_c:own_c + 256], T.w1[:]).then_inc(S.w_ld, 16)
+    g.scalar.dma_start(T.W[:, own_c + 256:own_c + 512], T.w2[:]).then_inc(S.w_ld, 16)
 
     ve.memset(T.ones[0:1, :], 1.0).then_inc(S.vin, 1)
-    ve.memset(T.G[:, 0:NS * 64], 0.0).then_inc(S.vin, 1)
+    ve.memset(T.G[0:1, 0:NG], 0.0).then_inc(S.vin, 1)
+    ve.memset(T.zi[:, 0:1], 1.0).then_inc(S.idm, 1)
+    ve.memset(T.zi[:, 1:129], 0.0).then_inc(S.idm, 1)
     ve.memset(T.zeros[:], 0.0).then_inc(S.zr, 1)
+    g.scalar.wait_ge(S.idm, 2)
+    g.scalar.dma_start(T.idd[:], T.zi[:]).then_inc(S.id1, 16)
+    g.scalar.wait_ge(S.id1, 16)
+    g.scalar.dma_start(T.ident[:], T.idd[0:128, :]).then_inc(S.id2, 16)
 
     sent = 0
     g.wait_ge(S.x_ld, 16)
     ks = list(range(1, NS))
     g.remote_dma_fused([RemoteDMATransfer(
         dst_ids=[dst_id(site_core[(s + k) % NS]) for k in ks], dma_engine_mask=off, remote_sem=S["xs%d" % s],
-        srcs=[T.X[:, 0:32]], dsts=[T.X[:, k * 32:(k + 1) * 32] for k in ks])], local_sem=S.sent)
+        srcs=[T.X[:, 0, :]], dsts=[T.X[:, k, :] for k in ks])], local_sem=S.sent)
     sent += n_off
     prid, ppid, _ = topo.addr(partner)
-    g.wait_ge(S.w1_ld, 16)
-    g.remote_dma(T.W1[:, own_c:own_c + 256], T.W1[:, own_c:own_c + 256], S.wp1, S.sent, ppid, prid, on)
+    g.wait_ge(S.w_ld, 32)
+    g.remote_dma(T.W[:, own_c:own_c + 512], T.W[:, own_c:own_c + 512], S.wp, S.sent, ppid, prid, on)
     sent += n_on
-    g.wait_ge(S.w2_ld, 16)
-    g.remote_dma(T.W2[:, own_c:own_c + 256], T.W2[:, own_c:own_c + 256], S.wp2, S.sent, ppid, prid, on)
-    sent += n_on
-    for sem, pair in ((S.cpE, (1, 2)), (S.cpF, (3, 4))):
+    for sem, pair in ((S.cp0, (1, 2)), (S.cp1, (3, 4))):
         g.wait_ge(sem, 1)
         g.remote_dma_fused([RemoteDMATransfer(
             dst_ids=[dst_id(site_core[(s - k) % NS])], dma_engine_mask=halves[q], remote_sem=S["rs%d" % s],
-            src=T.Z[:, k * 64:(k + 1) * 64], dst=T.R[:, s * 64:(s + 1) * 64]) for q, k in enumerate(pair)],
+            src=T.Z[:, k, :], dst=T.R[:, s * 64:(s + 1) * 64]) for q, k in enumerate(pair)],
             local_sem=S.sent)
         sent += 2 * n_half
-    g.wait_ge(S.cpG, 1)
+    g.wait_ge(S.cp2, 1)
     k = NS - 1
     rid, pid, _ = topo.addr(site_core[(s - k) % NS])
-    g.remote_dma(T.R[:, s * 64:(s + 1) * 64], T.Z[:, k * 64:(k + 1) * 64], S["rs%d" % s], S.sent, pid, rid, off)
+    g.remote_dma(T.R[:, s * 64:(s + 1) * 64], T.Z[:, k, :], S["rs%d" % s], S.sent, pid, rid, off)
     sent += n_off
     g.wait_ge(S.sent, sent)
 
@@ -165,88 +170,83 @@ def rank_program(g, core, T, topo):
     pe.wait_ge(S.vin, 2)
     pe.wait_ge(S.g_ld, 16)
     for (a, b, st), (c0, c1, d) in plan:
-        pe.matmul(T.G[:, c0:c1:d], T.ones[0:1, :], T.g1[0:1, a:b:st], True, True).then_inc(S.gdone, 1)
+        pe.matmul(T.G[0:1, c0:c1:d], T.ones[0:1, 0:1], T.g1[0:1, a:b:st], True, True).then_inc(S.gsc, 1)
+    ve.wait_ge(S.gsc, len(plan))
+    ve.tensor_copy(T.grow[0:1, :], T.G[0:1, 0:NG]).then_inc(S.gcp, 1)
+    pe.wait_ge(S.gcp, 1)
+    pe.matmul(T.G[:, 0:NG], T.ones[0:1, :], T.grow[0:1, :], True, True).then_inc(S.gdone, 1)
 
-    def mm1(H, col, wc, x0, n, sem):
-        for f in range(2):
-            pe.matmul(H[:, col + f * n:col + (f + 1) * n], T.W1[:, wc + f * 128:wc + (f + 1) * 128],
-                      T.X[:, x0:x0 + n], True, True).then_inc(sem, 1)
+    units = [((0, 1, 2), T.Ha, T.Za), ((3, 4), T.Hb, T.Zb), ((5,), T.Hc, T.Zc)]
+    experts = ((lane, own_c), (other, oth_c))
 
-    def mm2(Zp, zcol, wc, Hs, hcol, n, sem):
-        for f in range(2):
-            pe.matmul(Zp[:, zcol:zcol + 32], T.W2[:, wc + f * 128:wc + (f + 1) * 128],
-                      Hs[:, hcol + f * n:hcol + f * n + 32], f == 0, f == 1).then_inc(sem, 1)
+    def mm1(u):
+        slots, H, _ = units[u]
+        nk, k0 = len(slots), slots[0]
+        for k in slots:
+            if k:
+                pe.wait_ge(S["xs%d" % ((s - k) % NS)], n_off)
+            else:
+                pe.wait_ge(S.x_ld, 16)
+        for e, (j, wc) in enumerate(experts):
+            if u == 0 and e == 1:
+                pe.wait_ge(S.wp, n_on)
+            for f in range(2):
+                pe.matmul(H[:, (e * 2 + f) * nk:(e * 2 + f + 1) * nk, :], T.W[:, wc + f * 128:wc + (f + 1) * 128],
+                          T.X[:, k0:k0 + nk, :], True, True).then_inc(S["m1_%d" % u], 1)
 
-    pe.wait_ge(S.x_ld, 16)
-    pe.wait_ge(S.w1_ld, 16)
-    pe.wait_ge(S["xs%d" % ((s - 1) % NS)], n_off)
-    pe.wait_ge(S["xs%d" % ((s - 2) % NS)], n_off)
-    mm1(T.HA, 0, own_c, 0, 96, S.m1A)
-    pe.wait_ge(S.wp1, n_on)
-    mm1(T.HB, 0, oth_c, 0, 96, S.m1B)
-    pe.wait_ge(S.w2_ld, 16)
-    pe.wait_ge(S.rlA, 1)
-    for k in range(3):
-        mm2(T.ZE, k * 64 + lane * 32, own_c, T.HsA, k * 32, 96, S.m2E)
-    pe.wait_ge(S.wp2, n_on)
-    pe.wait_ge(S.rlB, 1)
-    for k in range(3):
-        mm2(T.ZE, k * 64 + other * 32, oth_c, T.HsB, k * 32, 96, S.m2E)
-    pe.wait_ge(S["xs%d" % ((s - 3) % NS)], n_off)
-    pe.wait_ge(S["xs%d" % ((s - 4) % NS)], n_off)
-    for j in range(2):
-        mm1(T.HC, j * 128, j * 256, 96, 64, S.m1C)
-    pe.wait_ge(S.rlC, 1)
-    for k in range(2):
-        for j in range(2):
-            mm2(T.ZF, k * 64 + j * 32, j * 256, T.HsC, j * 128 + k * 32, 64, S.m2F)
-    pe.wait_ge(S["xs%d" % ((s - 5) % NS)], n_off)
-    for j in range(2):
-        mm1(T.HD, j * 64, j * 256, 160, 32, S.m1D)
-    pe.wait_ge(S.rlD, 1)
-    for j in range(2):
-        mm2(T.ZG, j * 32, j * 256, T.HsD, j * 64, 32, S.m2G)
+    def mm2(u):
+        slots, _, Zp = units[u]
+        nk = len(slots)
+        pe.wait_ge(S["rl%d" % u], 1)
+        for e, (j, wc) in enumerate(experts):
+            for f in range(2):
+                hb = u * 12 + (e * 2 + f) * nk
+                pe.matmul(Zp[:, 0:nk, j * 32:(j + 1) * 32], T.W[:, wc + 256 + f * 128:wc + 256 + (f + 1) * 128],
+                          T.Hs[:, hb:hb + nk, :], f == 0, f == 1).then_inc(S["m2_%d" % u], 1)
 
-    MAX, MUL, ADD = AluOpType.max, AluOpType.mult, AluOpType.add
+    def relu(u):
+        slots, H, _ = units[u]
+        nb = 4 * len(slots)
+        ve.wait_ge(S["m1_%d" % u], 4)
+        ve.tensor_tensor(T.Hs[:, u * 12:u * 12 + nb, :], H[:, 0:nb, :], T.zeros[:, 0:nb, :], MAX).then_inc(S["rl%d" % u], 1)
+
+    def copy(u):
+        slots, _, Zp = units[u]
+        q0 = 1 if u == 0 else 0
+        ve.wait_ge(S["m2_%d" % u], 4)
+        ve.tensor_copy(T.Z[:, slots[q0]:slots[-1] + 1, :], Zp[:, q0:len(slots), :]).then_inc(S["cp%d" % u], 1)
+
+    pe.wait_ge(S.w_ld, 32)
+    mm1(0)
+    mm1(1)
+    mm2(0)
+    mm1(2)
+    mm2(1)
+    mm2(2)
     ve.wait_ge(S.zr, 1)
-    ve.wait_ge(S.m1A, 2)
-    ve.tensor_tensor(T.HsA[:], T.HA[:, 0:192], T.zeros[:, 0:192], MAX).then_inc(S.rlA, 1)
-    ve.wait_ge(S.m1B, 2)
-    ve.tensor_tensor(T.HsB[:], T.HB[:, 0:192], T.zeros[:, 0:192], MAX).then_inc(S.rlB, 1)
-    ve.wait_ge(S.m2E, 12)
-    ve.tensor_copy(T.Z[:, 64:192], T.ZE[:, 64:192]).then_inc(S.cpE, 1)
-    ve.tensor_copy(T.R[:, s * 64:(s + 1) * 64], T.ZE[:, 0:64]).then_inc(S.cp0, 1)
-    ve.wait_ge(S.m1C, 4)
-    ve.tensor_tensor(T.HsC[:], T.HC[:, 0:256], T.zeros[:, 0:256], MAX).then_inc(S.rlC, 1)
-    ve.wait_ge(S.m2F, 8)
-    ve.tensor_copy(T.Z[:, 192:320], T.ZF[:, 0:128]).then_inc(S.cpF, 1)
-    ve.wait_ge(S.m1D, 4)
-    ve.tensor_tensor(T.HsD[:], T.HD[:, 0:128], T.zeros[:, 0:128], MAX).then_inc(S.rlD, 1)
-    ve.wait_ge(S.m2G, 4)
-    ve.tensor_copy(T.Z[:, 320:384], T.ZG[:, 0:64]).then_inc(S.cpG, 1)
+    relu(0)
+    relu(1)
+    copy(0)
+    relu(2)
+    copy(1)
+    copy(2)
+    ve.tensor_copy(T.R[:, s * 64:(s + 1) * 64], T.Za[:, 0, :]).then_inc(S.cpown, 1)
 
-    ve.wait_ge(S.gdone, len(plan))
-    ve.wait_ge(S.cp0, 1)
+    ve.wait_ge(S.gdone, 1)
+    ve.wait_ge(S.cpown, 1)
+    pe.wait_ge(S.id2, 16)
     for k in range(NS):
         b = ((s + k) % NS) * 64
         if k:
             ve.wait_ge(S["rs%d" % ((s + k) % NS)], n_half if k < NS - 1 else n_off)
-        ve.tensor_tensor(T.P[:, k * 64:(k + 1) * 64], T.R[:, b:b + 64], T.G[:, b:b + 64], MUL).then_inc(S["pk%d" % k], 1)
-        ve.wait_ge(S["pk%d" % k], 1)
-        if 1 <= k < NS - 1:
-            prev = T.P[:, 0:64] if k == 1 else T.ACC[:, (k - 1) * 64:k * 64]
-            if k > 1:
-                ve.wait_ge(S["ac%d" % (k - 1)], 1)
-            ve.tensor_tensor(T.ACC[:, k * 64:(k + 1) * 64], prev, T.P[:, k * 64:(k + 1) * 64], ADD).then_inc(S["ac%d" % k], 1)
-        if k == NS - 2:
-            ve.wait_ge(S["ac%d" % k], 1)
-            ve.tensor_tensor(T.ACC[:, 0:32], T.ACC[:, k * 64:k * 64 + 32], T.ACC[:, k * 64 + 32:k * 64 + 64], ADD).then_inc(S.ac0, 1)
-    k = NS - 1
-    ve.tensor_tensor(T.ACC[:, 32:64], T.P[:, k * 64:k * 64 + 32], T.P[:, k * 64 + 32:k * 64 + 64], ADD).then_inc(S["ac%d" % k], 1)
-    ve.wait_ge(S["ac%d" % k], 1)
-    ve.wait_ge(S.ac0, 1)
-    ve.tensor_tensor(T.Y[:], T.ACC[:, 0:32], T.ACC[:, 32:64], ADD).then_inc(S["ac%d" % NS], 1)
+        ve.tensor_tensor(T.M[:, b:b + 64], T.R[:, b:b + 64], T.G[:, b:b + 64], MUL).then_inc(S["pk%d" % k], 1)
+        pe.wait_ge(S["pk%d" % k], 1)
+        for j in range(2):
+            pe.matmul(T.AC[:, 0:32], T.ident[:], T.M[:, b + j * 32:b + (j + 1) * 32],
+                      k == 0 and j == 0, k == NS - 1 and j == 1).then_inc(S.acc, 1)
+    ve.wait_ge(S.acc, 2 * NS)
+    ve.tensor_copy(T.Y[:], T.AC[:, 0:32]).then_inc(S.yy, 1)
 
-    g.sync.wait_ge(S["ac%d" % NS], 1)
+    g.sync.wait_ge(S.yy, 1)
     g.sync.dma_start(T.y[:], T.Y[:]).then_inc(S.y_st, 16)
     g.sync.wait_ge(S.y_st, 16)

from concourse.bass import DstId, RemoteDMATransfer
from concourse.mybir import AluOpType

NS = 6
TOKS = 32
NU = 3

SCRATCH = {
    "X": ("sbuf", [128, NS, 32], "bfloat16"),
    "W": ("sbuf", [128, 1024], "bfloat16"),
    "g1": ("sbuf", [128, 96], "bfloat16"),
    "grow": ("sbuf", [128, NS * 64], "bfloat16"),
    "ones": ("sbuf", [128, 128], "bfloat16"),
    "zeros": ("sbuf", [128, 12, 32], "float32"),
    "zi": ("sbuf", [128, 129], "bfloat16"),
    "idd": ("dram", [129, 128], "bfloat16"),
    "ident": ("sbuf", [128, 128], "bfloat16"),
    "Hs": ("sbuf", [128, NU * 12, 32], "bfloat16"),
    "Z": ("sbuf", [128, NS, 64], "bfloat16"),
    "R": ("sbuf", [128, NS * 64], "bfloat16"),
    "M": ("sbuf", [128, NS * 64], "bfloat16"),
    "Y": ("sbuf", [128, 32], "bfloat16"),
    "G": ("psum", [128, 512], "float32"),
    "Ha": ("psum", [128, 16, 32], "float32"),
    "Hb": ("psum", [128, 16, 32], "float32"),
    "Hc": ("psum", [128, 16, 32], "float32"),
    "Za": ("psum", [128, 8, 64], "float32"),
    "Zb": ("psum", [128, 8, 64], "float32"),
    "Zc": ("psum", [128, 8, 64], "float32"),
    "AC": ("psum", [128, 512], "float32"),
}
SEMAPHORES = (["x_ld", "w_ld", "g_ld", "y_st", "vin", "zr", "idm", "id1", "id2", "gsc", "gcp", "gdone", "wp", "sent",
               "cpown", "acc", "yy"]
              + ["%s%d" % (n, u) for n in ("m1_", "rl", "m2_", "cp") for u in range(NU)]
              + ["xs%d" % i for i in range(NS)] + ["rs%d" % i for i in range(NS)]
              + ["pk%d" % i for i in range(NS)])


def _bits(mask):
    return [b for b in range(16) if (mask >> b) & 1]


def _mk(bits):
    m = 0
    for b in bits:
        m |= 1 << b
    return m


def _layout(T, topo):
    chips = sorted(set(topo.chip(c) for c in T.cores))
    first = [c for c in T.cores if topo.chip(c) == chips[0]]
    dies = [topo.die(c) for c in first]
    members = []
    for ch in chips:
        row = [None] * len(dies)
        for r, c in enumerate(T.cores):
            if topo.chip(c) == ch:
                row[dies.index(topo.die(c))] = r
        members.append(row)
    return members


def _scatter_plan(route_r, blk):
    plan, singles = [], {}
    for t, es in enumerate(route_r):
        c = [blk[e] * TOKS + t for e in es]
        d0, d1 = c[1] - c[0], c[2] - c[1]
        if d0 == d1 and d0 > 0:
            plan.append(((t, t + 65, 32), (c[0], c[2] + 1, d0)))
        elif d0 > 0:
            plan.append(((t, t + 33, 32), (c[0], c[1] + 1, d0)))
            singles[(2, t)] = c[2]
        elif d1 > 0:
            plan.append(((32 + t, 32 + t + 33, 32), (c[1], c[2] + 1, d1)))
            singles[(0, t)] = c[0]
        else:
            for i in range(3):
                singles[(i, t)] = c[i]
    done = set()
    for (i, t) in sorted(singles):
        if (i, t) in done:
            continue
        n = 1
        while (i, t + n) in singles and singles[(i, t + n)] == singles[(i, t)] + n:
            n += 1
        for q in range(n):
            done.add((i, t + q))
        plan.append(((i * 32 + t, i * 32 + t + n, 1), (singles[(i, t)], singles[(i, t)] + n, 1)))
    return plan


def rank_program(g, core, T, topo):
    rank = T.rank_of(core)
    if rank is None:
        return
    S = T.sem
    pe, ve = g.tensor, g.vector
    members = _layout(T, topo)
    s = [i for i, row in enumerate(members) if rank in row][0]
    lane = members[s].index(rank)
    other = 1 - lane
    partner = T.cores[members[s][other]]
    blk = {}
    for i, row in enumerate(members):
        for j, r in enumerate(row):
            blk[r] = i * 2 + j
    site_core = [T.cores[members[i][lane]] for i in range(NS)]

    off = topo.mask(core, partner)
    for i in range(NS):
        if i != s:
            off &= topo.mask(core, site_core[i])
    on = topo.mask(core, partner) & ~off
    if on == 0:
        on = topo.mask(core, partner)
    ob = _bits(off)
    halves = [_mk(ob[:len(ob) // 2]), _mk(ob[len(ob) // 2:])]
    n_off, n_on, n_half = len(ob), len(_bits(on)), len(ob) // 2

    def dst_id(c):
        rid, pid, _ = topo.addr(c)
        return DstId(rid=rid, pnc=pid)

    own_c, oth_c = lane * 512, other * 512
    MAX, MUL = AluOpType.max, AluOpType.mult
    NG = NS * 64

    g.sync.dma_start(T.X[:, 0, :], T.x[:]).then_inc(S.x_ld, 16)
    g.scalar.dma_start(T.g1[0:1, :], T.gate[:]).then_inc(S.g_ld, 16)
    g.sync.dma_start(T.W[:, own_c:own_c + 256], T.w1[:]).then_inc(S.w_ld, 16)
    g.scalar.dma_start(T.W[:, own_c + 256:own_c + 512], T.w2[:]).then_inc(S.w_ld, 16)

    ve.memset(T.ones[0:1, :], 1.0).then_inc(S.vin, 1)
    ve.memset(T.G[0:1, 0:NG], 0.0).then_inc(S.vin, 1)
    ve.memset(T.zi[:, 0:1], 1.0).then_inc(S.idm, 1)
    ve.memset(T.zi[:, 1:129], 0.0).then_inc(S.idm, 1)
    ve.memset(T.zeros[:], 0.0).then_inc(S.zr, 1)
    g.scalar.wait_ge(S.idm, 2)
    g.scalar.dma_start(T.idd[:], T.zi[:]).then_inc(S.id1, 16)
    g.scalar.wait_ge(S.id1, 16)
    g.scalar.dma_start(T.ident[:], T.idd[0:128, :]).then_inc(S.id2, 16)

    sent = 0
    g.wait_ge(S.x_ld, 16)
    ks = list(range(1, NS))
    g.remote_dma_fused([RemoteDMATransfer(
        dst_ids=[dst_id(site_core[(s + k) % NS]) for k in ks], dma_engine_mask=off, remote_sem=S["xs%d" % s],
        srcs=[T.X[:, 0, :]], dsts=[T.X[:, k, :] for k in ks])], local_sem=S.sent)
    sent += n_off
    prid, ppid, _ = topo.addr(partner)
    g.wait_ge(S.w_ld, 32)
    g.remote_dma(T.W[:, own_c:own_c + 512], T.W[:, own_c:own_c + 512], S.wp, S.sent, ppid, prid, on)
    sent += n_on
    for sem, pair in ((S.cp0, (1, 2)), (S.cp1, (3, 4))):
        g.wait_ge(sem, 1)
        g.remote_dma_fused([RemoteDMATransfer(
            dst_ids=[dst_id(site_core[(s - k) % NS])], dma_engine_mask=halves[q], remote_sem=S["rs%d" % s],
            src=T.Z[:, k, :], dst=T.R[:, s * 64:(s + 1) * 64]) for q, k in enumerate(pair)],
            local_sem=S.sent)
        sent += 2 * n_half
    g.wait_ge(S.cp2, 1)
    k = NS - 1
    rid, pid, _ = topo.addr(site_core[(s - k) % NS])
    g.remote_dma(T.R[:, s * 64:(s + 1) * 64], T.Z[:, k, :], S["rs%d" % s], S.sent, pid, rid, off)
    sent += n_off
    g.wait_ge(S.sent, sent)

    plan = _scatter_plan(T.tables["ROUTE"][rank], blk)
    pe.wait_ge(S.vin, 2)
    pe.wait_ge(S.g_ld, 16)
    for (a, b, st), (c0, c1, d) in plan:
        pe.matmul(T.G[0:1, c0:c1:d], T.ones[0:1, 0:1], T.g1[0:1, a:b:st], True, True).then_inc(S.gsc, 1)
    ve.wait_ge(S.gsc, len(plan))
    ve.tensor_copy(T.grow[0:1, :], T.G[0:1, 0:NG]).then_inc(S.gcp, 1)
    pe.wait_ge(S.gcp, 1)
    pe.matmul(T.G[:, 0:NG], T.ones[0:1, :], T.grow[0:1, :], True, True).then_inc(S.gdone, 1)

    units = [((0, 1, 2), T.Ha, T.Za), ((3, 4), T.Hb, T.Zb), ((5,), T.Hc, T.Zc)]
    experts = ((lane, own_c), (other, oth_c))

    def mm1(u):
        slots, H, _ = units[u]
        nk, k0 = len(slots), slots[0]
        for k in slots:
            if k:
                pe.wait_ge(S["xs%d" % ((s - k) % NS)], n_off)
            else:
                pe.wait_ge(S.x_ld, 16)
        for e, (j, wc) in enumerate(experts):
            if u == 0 and e == 1:
                pe.wait_ge(S.wp, n_on)
            for f in range(2):
                pe.matmul(H[:, (e * 2 + f) * nk:(e * 2 + f + 1) * nk, :], T.W[:, wc + f * 128:wc + (f + 1) * 128],
                          T.X[:, k0:k0 + nk, :], True, True).then_inc(S["m1_%d" % u], 1)

    def mm2(u):
        slots, _, Zp = units[u]
        nk = len(slots)
        pe.wait_ge(S["rl%d" % u], 1)
        for e, (j, wc) in enumerate(experts):
            for f in range(2):
                hb = u * 12 + (e * 2 + f) * nk
                pe.matmul(Zp[:, 0:nk, j * 32:(j + 1) * 32], T.W[:, wc + 256 + f * 128:wc + 256 + (f + 1) * 128],
                          T.Hs[:, hb:hb + nk, :], f == 0, f == 1).then_inc(S["m2_%d" % u], 1)

    def relu(u):
        slots, H, _ = units[u]
        nb = 4 * len(slots)
        ve.wait_ge(S["m1_%d" % u], 4)
        ve.tensor_tensor(T.Hs[:, u * 12:u * 12 + nb, :], H[:, 0:nb, :], T.zeros[:, 0:nb, :], MAX).then_inc(S["rl%d" % u], 1)

    def copy(u):
        slots, _, Zp = units[u]
        q0 = 1 if u == 0 else 0
        ve.wait_ge(S["m2_%d" % u], 4)
        ve.tensor_copy(T.Z[:, slots[q0]:slots[-1] + 1, :], Zp[:, q0:len(slots), :]).then_inc(S["cp%d" % u], 1)

    pe.wait_ge(S.w_ld, 32)
    mm1(0)
    mm1(1)
    mm2(0)
    mm1(2)
    mm2(1)
    mm2(2)
    ve.wait_ge(S.zr, 1)
    relu(0)
    relu(1)
    copy(0)
    relu(2)
    copy(1)
    copy(2)
    ve.tensor_copy(T.R[:, s * 64:(s + 1) * 64], T.Za[:, 0, :]).then_inc(S.cpown, 1)

    ve.wait_ge(S.gdone, 1)
    ve.wait_ge(S.cpown, 1)
    pe.wait_ge(S.id2, 16)
    for k in range(NS):
        b = ((s + k) % NS) * 64
        if k:
            ve.wait_ge(S["rs%d" % ((s + k) % NS)], n_half if k < NS - 1 else n_off)
        ve.tensor_tensor(T.M[:, b:b + 64], T.R[:, b:b + 64], T.G[:, b:b + 64], MUL).then_inc(S["pk%d" % k], 1)
        pe.wait_ge(S["pk%d" % k], 1)
        for j in range(2):
            pe.matmul(T.AC[:, 0:32], T.ident[:], T.M[:, b + j * 32:b + (j + 1) * 32],
                      k == 0 and j == 0, k == NS - 1 and j == 1).then_inc(S.acc, 1)
    ve.wait_ge(S.acc, 2 * NS)
    ve.tensor_copy(T.Y[:], T.AC[:, 0:32]).then_inc(S.yy, 1)

    g.sync.wait_ge(S.yy, 1)
    g.sync.dma_start(T.y[:], T.Y[:]).then_inc(S.y_st, 16)
    g.sync.wait_ge(S.y_st, 16)
